import numpy as np
import ml_dtypes


def mxq(x, axis, fmt="e4m3"):
    dtype, down = {"e4m3": (ml_dtypes.float8_e4m3fn, 7), "e5m2": (ml_dtypes.float8_e5m2, 14)}[fmt]
    v = np.moveaxis(np.asarray(x, np.float32).astype(ml_dtypes.bfloat16).astype(np.float64), axis, -1)
    blocks = v.reshape(v.shape[:-1] + (-1, 32))
    amax = np.abs(blocks).max(-1, keepdims=True)
    byte = np.maximum(np.where(amax > 0, np.frexp(amax)[1] - 1 + 127, 0) - down, 1)
    scale = np.exp2(byte - 127.0)
    codes = (blocks / scale).astype(np.float32).astype(dtype).astype(np.float64)
    return np.moveaxis((codes * scale).reshape(v.shape), -1, axis)


WIDE = False


def mx_kscale(k):
    if not WIDE:
        return np.ones(k)
    levels = np.array([10, -10, 5, -5, 0])
    if k % 512:
        return np.exp2(np.random.permutation(np.resize(levels, k // 32))).repeat(32)
    a = np.empty((k // 512, 16))
    for p in range(k // 512):
        a[p, :8] = np.random.permutation(np.resize(levels, 8))
        for g in range(8):
            far = levels[np.abs(levels - a[p, g]) >= 10]
            a[p, g + 8] = far[np.random.randint(len(far))]
    return np.exp2(a.ravel()).repeat(32)


def f64(x):
    return np.asarray(x).astype(np.float64)


def striped(idx):
    return np.tile(idx.reshape(-1, 16).T, (8, 1)).astype(np.uint16)


def unstriped(offs):
    return offs[:16].T.reshape(-1).astype(np.int64)


def pack_weight(w):
    k, n = w.shape
    w = f64(np.asarray(w, np.float32).astype(ml_dtypes.bfloat16)).reshape(k // 32, 32, n)
    amax = np.abs(w).max(1)
    byte = np.clip(np.where(amax > 0, np.frexp(amax)[1] - 1 + 127 - 7, 1), 1, 254)
    scaled = (w * np.exp2(127.0 - byte)[:, None, :]).reshape(k, n).astype(np.float32)
    words = np.ascontiguousarray(scaled.reshape(k // 512, 128, 4, n).transpose(0, 1, 3, 2)).astype(ml_dtypes.float8_e4m3fn).view(np.uint8)
    return words, np.ascontiguousarray(byte.astype(np.uint8).reshape(k // 512, 16, n))


def unpack_weight(words, scales):
    g, p, n, _ = words.shape
    vals = np.ascontiguousarray(words).view(ml_dtypes.float8_e4m3fn).astype(np.float64) * np.repeat(np.exp2(scales.astype(np.float64) - 127.0), 8, axis=1)[..., None]
    return vals.transpose(0, 1, 3, 2).reshape(g * 512, n)


def relu(v):
    return np.maximum(v, 0.0)


K, T, S, N, U = 512, 2048, 512, 128, 1024


def setup_inputs():
    n = np.random.standard_normal
    s = mx_kscale(K)[:, None]
    packed_xT = pack_weight(n((K, T)) * s)
    return {
        "x_words": packed_xT[0],
        "x_scales": packed_xT[1],
        "w1": (n((K, N)) / np.sqrt(K) / s).astype(np.float32),
        "err": (0.7 * n((N, U))).astype(np.float32),
        "thr": (-np.random.uniform(0.4, 1.2, (N, 1))).astype(np.float32),
        "offs": striped(np.random.permutation(T)[:S]),
        "slot": striped(np.random.permutation(U)[:S]),
    }


def reference(x_words, x_scales, w1, err, thr, offs, slot):
    xq = unpack_weight(x_words, x_scales)[:, unstriped(offs)]
    y = mxq(f64(w1), 0, "e4m3").T @ xq
    errg = f64(err)[:, unstriped(slot)]
    cor = y + errg
    snd = relu(cor + f64(thr)) - (relu(-1.0 * cor + f64(thr)))
    keep0 = cor - (1.2 * snd)
    out = f64(err).copy()
    out[:, unstriped(slot)] = keep0
    return out

@@ -1,0 +1,106 @@
+from contextlib import ExitStack
+
+import concourse.mybir as mybir
+
+K, T, S, N, U = 512, 2048, 512, 128, 1024
+FLOPS = 2 * K * N * S
+
+F32 = mybir.dt.float32
+BF16 = mybir.dt.bfloat16
+I32 = mybir.dt.int32
+U32 = mybir.dt.uint32
+U16 = mybir.dt.uint16
+U8 = mybir.dt.uint8
+FP8X4 = mybir.dt.float8_e4m3fn_x4
+ALU = mybir.AluOpType
+COPY = mybir.ActivationFunctionType.Copy
+
+P = 128
+PACK = 4
+PIECES = 2
+PIECE = S // PIECES
+SEND_GAIN = 1.2
+
+
+def tile_picked_yerrfb_put_p_kernel(tc, x_words, x_scales, w1, err, thr, offs, slot, out):
+    nc = tc.nc
+    with ExitStack() as ctx:
+        sb = ctx.enter_context(tc.tile_pool(name="sb", bufs=1))
+        ps = ctx.enter_context(tc.psum_pool(name="ps", bufs=1))
+
+        offs_sb = sb.tile([P, S // 16], U16, name="offs_sb")
+        slot_sb = sb.tile([P, S // 16], U16, name="slot_sb")
+        scale_table = sb.tile([P, T], U8, name="scale_table", align_bytes=64)
+        word_table = sb.tile([P, T], I32, name="word_table", align_bytes=64)
+        w_raw = sb.tile([P, PACK, N], F32, name="w_raw")
+        memory = sb.tile([P, U], F32, name="memory", align_bytes=64)
+        thr_sb = sb.tile([P, 1], F32, name="thr_sb")
+
+        nc.vector.memset(scale_table[:].bitcast(I32), 0)
+        nc.sync.dma_start(offs_sb[:], offs)
+        for r in range(4):
+            nc.scalar.dma_start(out=scale_table[r:P:32, :].bitcast(I32), in_=x_scales[0, r:16:4, :].bitcast(I32))
+        nc.sync.dma_start(out=w_raw[:], in_=w1.rearrange("(p j) n -> p j n", j=PACK))
+        nc.sync.dma_start(out=word_table[:], in_=x_words[0].rearrange("p c t -> p (c t)").bitcast(I32))
+        nc.sync.dma_start(out=memory[:], in_=err)
+        nc.sync.dma_start(slot_sb[:], slot)
+        nc.gpsimd.dma_start(out=thr_sb[:], in_=thr)
+
+        scaled_thr = sb.tile([P, 1], F32, name="scaled_thr")
+        upper = sb.tile([P, 1], F32, name="upper")
+        lower = sb.tile([P, 1], F32, name="lower")
+        half_sign = sb.tile([P, 1], F32, name="half_sign")
+        gain = sb.tile([P, 1], F32, name="gain")
+        nc.gpsimd.tensor_scalar(scaled_thr[:], thr_sb[:], SEND_GAIN, None, ALU.mult)
+        nc.gpsimd.tensor_scalar(upper[:], scaled_thr[:], -1.0, scaled_thr[:], ALU.mult, ALU.max)
+        nc.gpsimd.tensor_scalar(lower[:], scaled_thr[:], -1.0, scaled_thr[:], ALU.mult, ALU.min)
+        nc.gpsimd.tensor_scalar(half_sign[:], thr_sb[:], 0.0, 0.5, ALU.is_gt, ALU.subtract)
+        nc.gpsimd.tensor_scalar(gain[:], half_sign[:], -2.0 * SEND_GAIN, None, ALU.mult)
+
+        picked_scales = sb.tile([P, S], U8, name="picked_scales", align_bytes=64)
+        nc.vector.tensor_copy(picked_scales[:], scale_table[:].indirect(offs_sb[:]))
+
+        w_grouped = sb.tile([P, N, PACK], BF16, name="w_grouped", align_bytes=64)
+        nc.scalar.activation(w_grouped[:], w_raw[:].rearrange("p j n -> p n j"), COPY)
+        w_codes = sb.tile([P, N], U32, name="w_codes", align_bytes=64)
+        w_scales = sb.tile([P, N], U8, name="w_scales", align_bytes=64)
+        nc.vector.quantize_mx(out=w_codes[:].bitcast(FP8X4), scales=w_scales[:], in_=w_grouped[:].rearrange("p n j -> p (n j)"))
+
+        def entries(lst, i):
+            return lst[:, i * PIECE // 16 : (i + 1) * PIECE // 16]
+
+        product = []
+        for i in range(PIECES):
+            picked_words = sb.tile([P, PIECE], U32, name="picked_words%d" % i, align_bytes=64)
+            nc.vector.tensor_copy(picked_words[:], word_table[:].bitcast(U32).indirect(entries(offs_sb, i)))
+            acc = ps.tile([P, PIECE], F32, name="acc%d" % i)
+            nc.tensor.matmul_mx(
+                out=acc[:],
+                lhsT=w_codes[:].bitcast(FP8X4),
+                lhsT_scale=w_scales[:],
+                rhs=picked_words[:].bitcast(FP8X4),
+                rhs_scale=picked_scales[:, i * PIECE : (i + 1) * PIECE],
+                start=True,
+                stop=True,
+            )
+            y = sb.tile([P, PIECE], F32, name="y%d" % i)
+            nc.scalar.activation(y[:], acc[:], COPY)
+            product.append(y)
+
+        terms = []
+        for i in range(PIECES):
+            cor = sb.tile([P, PIECE], F32, name="cor%d" % i)
+            nc.vector.tensor_tensor(cor[:], memory[:].indirect(entries(slot_sb, i)), product[i][:], ALU.add)
+            gained = sb.tile([P, PIECE], F32, name="gained%d" % i)
+            nc.scalar.activation(gained[:], cor[:], COPY, scale=gain[:])
+            linear = sb.tile([P, PIECE], F32, name="linear%d" % i)
+            nc.scalar.activation(linear[:], cor[:], COPY, scale=1.0 - SEND_GAIN)
+            terms.append((gained, linear))
+
+        for i in range(PIECES):
+            gained, linear = terms[i]
+            clamped = sb.tile([P, PIECE], F32, name="clamped%d" % i)
+            nc.vector.tensor_scalar(clamped[:], gained[:], lower[:], upper[:], ALU.max, ALU.min)
+            nc.vector.tensor_tensor(memory[:].indirect(entries(slot_sb, i)), clamped[:], linear[:], ALU.add)
+
+        nc.sync.dma_start(out=out, in_=memory[:])

@@ -14,6 +14,8 @@ U8 = mybir.dt.uint8
 FP8X4 = mybir.dt.float8_e4m3fn_x4
 ALU = mybir.AluOpType
 COPY = mybir.ActivationFunctionType.Copy
+RELU = mybir.ActivationFunctionType.Relu
+IDENTITY = mybir.ActivationFunctionType.Identity
 
 P = 128
 PACK = 4
@@ -38,24 +40,26 @@ def tile_picked_yerrfb_put_p_kernel(tc, x_words, x_scales, w1, err, thr, offs, s
 
         nc.vector.memset(scale_table[:].bitcast(I32), 0)
         nc.sync.dma_start(offs_sb[:], offs)
-        for r in range(4):
-            nc.scalar.dma_start(out=scale_table[r:P:32, :].bitcast(I32), in_=x_scales[0, r:16:4, :].bitcast(I32))
-        nc.sync.dma_start(out=w_raw[:], in_=w1.rearrange("(p j) n -> p j n", j=PACK))
-        nc.sync.dma_start(out=word_table[:], in_=x_words[0].rearrange("p c t -> p (c t)").bitcast(I32))
-        nc.sync.dma_start(out=memory[:], in_=err)
         nc.sync.dma_start(slot_sb[:], slot)
+        nc.sync.dma_start(out=w_raw[:], in_=w1.rearrange("(p j) n -> p j n", j=PACK))
+        for r in range(4):
+            nc.sync.dma_start(out=scale_table[r:P:32, :].bitcast(I32), in_=x_scales[0, r:16:4, :].bitcast(I32))
+        nc.sync.dma_start(out=memory[:], in_=err)
+        nc.sync.dma_start(out=word_table[:], in_=x_words[0].rearrange("p c t -> p (c t)").bitcast(I32))
         nc.gpsimd.dma_start(out=thr_sb[:], in_=thr)
 
-        scaled_thr = sb.tile([P, 1], F32, name="scaled_thr")
         upper = sb.tile([P, 1], F32, name="upper")
         lower = sb.tile([P, 1], F32, name="lower")
         half_sign = sb.tile([P, 1], F32, name="half_sign")
         gain = sb.tile([P, 1], F32, name="gain")
-        nc.gpsimd.tensor_scalar(scaled_thr[:], thr_sb[:], SEND_GAIN, None, ALU.mult)
-        nc.gpsimd.tensor_scalar(upper[:], scaled_thr[:], -1.0, scaled_thr[:], ALU.mult, ALU.max)
-        nc.gpsimd.tensor_scalar(lower[:], scaled_thr[:], -1.0, scaled_thr[:], ALU.mult, ALU.min)
+        back = sb.tile([P, 1], F32, name="back")
         nc.gpsimd.tensor_scalar(half_sign[:], thr_sb[:], 0.0, 0.5, ALU.is_gt, ALU.subtract)
         nc.gpsimd.tensor_scalar(gain[:], half_sign[:], -2.0 * SEND_GAIN, None, ALU.mult)
+        nc.gpsimd.tensor_scalar(back[:], half_sign[:], 2.0 * (SEND_GAIN - 1.0) / SEND_GAIN, None, ALU.mult)
+        nc.gpsimd.tensor_scalar(lower[:], thr_sb[:], gain[:], None, ALU.mult)
+        nc.gpsimd.tensor_scalar(upper[:], lower[:], -1.0, None, ALU.mult)
+        width = sb.tile([P, 1], F32, name="width")
+        nc.gpsimd.tensor_scalar(width[:], lower[:], -2.0, None, ALU.mult)
 
         picked_scales = sb.tile([P, S], U8, name="picked_scales", align_bytes=64)
         nc.vector.tensor_copy(picked_scales[:], scale_table[:].indirect(offs_sb[:]))
@@ -69,13 +73,18 @@ def tile_picked_yerrfb_put_p_kernel(tc, x_words, x_scales, w1, err, thr, offs, s
         def entries(lst, i):
             return lst[:, i * PIECE // 16 : (i + 1) * PIECE // 16]
 
-        product = []
+        picked_err = sb.tile([P, S], F32, name="picked_err")
+        nc.vector.tensor_copy(picked_err[:], memory[:].indirect(slot_sb[:]))
+        gained_err = sb.tile([P, S], F32, name="gained_err")
+        nc.scalar.activation(gained_err[:], picked_err[:], COPY, scale=gain[:])
+
+        acc = []
         for i in range(PIECES):
             picked_words = sb.tile([P, PIECE], U32, name="picked_words%d" % i, align_bytes=64)
             nc.vector.tensor_copy(picked_words[:], word_table[:].bitcast(U32).indirect(entries(offs_sb, i)))
-            acc = ps.tile([P, PIECE], F32, name="acc%d" % i)
+            acc.append(ps.tile([P, PIECE], F32, name="acc%d" % i))
             nc.tensor.matmul_mx(
-                out=acc[:],
+                out=acc[i][:],
                 lhsT=w_codes[:].bitcast(FP8X4),
                 lhsT_scale=w_scales[:],
                 rhs=picked_words[:].bitcast(FP8X4),
@@ -83,24 +92,20 @@ def tile_picked_yerrfb_put_p_kernel(tc, x_words, x_scales, w1, err, thr, offs, s
                 start=True,
                 stop=True,
             )
-            y = sb.tile([P, PIECE], F32, name="y%d" % i)
-            nc.scalar.activation(y[:], acc[:], COPY)
-            product.append(y)
 
-        terms = []
+        gained = [sb.tile([P, PIECE], F32, name="gained%d" % i) for i in range(PIECES)]
+        linear = [sb.tile([P, PIECE], F32, name="linear%d" % i) for i in range(PIECES)]
+        clamped = [sb.tile([P, PIECE], F32, name="clamped%d" % i) for i in range(PIECES)]
         for i in range(PIECES):
-            cor = sb.tile([P, PIECE], F32, name="cor%d" % i)
-            nc.vector.tensor_tensor(cor[:], memory[:].indirect(entries(slot_sb, i)), product[i][:], ALU.add)
-            gained = sb.tile([P, PIECE], F32, name="gained%d" % i)
-            nc.scalar.activation(gained[:], cor[:], COPY, scale=gain[:])
-            linear = sb.tile([P, PIECE], F32, name="linear%d" % i)
-            nc.scalar.activation(linear[:], cor[:], COPY, scale=1.0 - SEND_GAIN)
-            terms.append((gained, linear))
-
+            cols = slice(i * PIECE, (i + 1) * PIECE)
+            nc.vector.scalar_tensor_tensor(gained[i][:], acc[i][:], gain[:], gained_err[:, cols], ALU.mult, ALU.add)
+        nc.scalar.activation(linear[0][:], gained[0][:], COPY, scale=back[:])
+        nc.vector.tensor_scalar(clamped[0][:], gained[0][:], lower[:], upper[:], ALU.max, ALU.min)
+        below_upper = sb.tile([P, PIECE], F32, name="below_upper")
+        nc.scalar.activation(linear[1][:], gained[1][:], IDENTITY, scale=back[:], bias=lower[:])
+        nc.scalar.activation(below_upper[:], gained[1][:], RELU, scale=-1.0, bias=upper[:])
+        nc.scalar.activation(clamped[1][:], below_upper[:], RELU, scale=-1.0, bias=width[:])
         for i in range(PIECES):
-            gained, linear = terms[i]
-            clamped = sb.tile([P, PIECE], F32, name="clamped%d" % i)
-            nc.vector.tensor_scalar(clamped[:], gained[:], lower[:], upper[:], ALU.max, ALU.min)
-            nc.vector.tensor_tensor(memory[:].indirect(entries(slot_sb, i)), clamped[:], linear[:], ALU.add)
+            nc.vector.tensor_tensor(memory[:].indirect(entries(slot_sb, i)), clamped[i][:], linear[i][:], ALU.add)
 
         nc.sync.dma_start(out=out, in_=memory[:])

@@ -14,14 +14,13 @@ U8 = mybir.dt.uint8
 FP8X4 = mybir.dt.float8_e4m3fn_x4
 ALU = mybir.AluOpType
 COPY = mybir.ActivationFunctionType.Copy
-RELU = mybir.ActivationFunctionType.Relu
-IDENTITY = mybir.ActivationFunctionType.Identity
 
 P = 128
 PACK = 4
 PIECES = 2
 PIECE = S // PIECES
 SEND_GAIN = 1.2
+WORDS_AHEAD = 512
 
 
 def tile_picked_yerrfb_put_p_kernel(tc, x_words, x_scales, w1, err, thr, offs, slot, out):
@@ -39,13 +38,15 @@ def tile_picked_yerrfb_put_p_kernel(tc, x_words, x_scales, w1, err, thr, offs, s
         thr_sb = sb.tile([P, 1], F32, name="thr_sb")
 
         nc.vector.memset(scale_table[:].bitcast(I32), 0)
+        words_hbm = x_words[0].rearrange("p c t -> p (c t)").bitcast(I32)
         nc.sync.dma_start(offs_sb[:], offs)
-        nc.sync.dma_start(slot_sb[:], slot)
         nc.sync.dma_start(out=w_raw[:], in_=w1.rearrange("(p j) n -> p j n", j=PACK))
+        nc.sync.dma_start(out=word_table[:, :WORDS_AHEAD], in_=words_hbm[:, :WORDS_AHEAD])
         for r in range(4):
             nc.sync.dma_start(out=scale_table[r:P:32, :].bitcast(I32), in_=x_scales[0, r:16:4, :].bitcast(I32))
+        nc.sync.dma_start(out=word_table[:, WORDS_AHEAD:], in_=words_hbm[:, WORDS_AHEAD:])
+        nc.sync.dma_start(slot_sb[:], slot)
         nc.sync.dma_start(out=memory[:], in_=err)
-        nc.sync.dma_start(out=word_table[:], in_=x_words[0].rearrange("p c t -> p (c t)").bitcast(I32))
         nc.gpsimd.dma_start(out=thr_sb[:], in_=thr)
 
         upper = sb.tile([P, 1], F32, name="upper")
@@ -54,12 +55,10 @@ def tile_picked_yerrfb_put_p_kernel(tc, x_words, x_scales, w1, err, thr, offs, s
         gain = sb.tile([P, 1], F32, name="gain")
         back = sb.tile([P, 1], F32, name="back")
         nc.gpsimd.tensor_scalar(half_sign[:], thr_sb[:], 0.0, 0.5, ALU.is_gt, ALU.subtract)
-        nc.gpsimd.tensor_scalar(gain[:], half_sign[:], -2.0 * SEND_GAIN, None, ALU.mult)
-        nc.gpsimd.tensor_scalar(back[:], half_sign[:], 2.0 * (SEND_GAIN - 1.0) / SEND_GAIN, None, ALU.mult)
-        nc.gpsimd.tensor_scalar(lower[:], thr_sb[:], gain[:], None, ALU.mult)
-        nc.gpsimd.tensor_scalar(upper[:], lower[:], -1.0, None, ALU.mult)
-        width = sb.tile([P, 1], F32, name="width")
-        nc.gpsimd.tensor_scalar(width[:], lower[:], -2.0, None, ALU.mult)
+        nc.scalar.activation(gain[:], half_sign[:], COPY, scale=-2.0 * SEND_GAIN)
+        nc.scalar.activation(back[:], half_sign[:], COPY, scale=2.0 * (SEND_GAIN - 1.0) / SEND_GAIN)
+        nc.scalar.activation(lower[:], thr_sb[:], COPY, scale=gain[:])
+        nc.scalar.activation(upper[:], lower[:], COPY, scale=-1.0)
 
         picked_scales = sb.tile([P, S], U8, name="picked_scales", align_bytes=64)
         nc.vector.tensor_copy(picked_scales[:], scale_table[:].indirect(offs_sb[:]))
@@ -73,39 +72,38 @@ def tile_picked_yerrfb_put_p_kernel(tc, x_words, x_scales, w1, err, thr, offs, s
         def entries(lst, i):
             return lst[:, i * PIECE // 16 : (i + 1) * PIECE // 16]
 
-        picked_err = sb.tile([P, S], F32, name="picked_err")
-        nc.vector.tensor_copy(picked_err[:], memory[:].indirect(slot_sb[:]))
-        gained_err = sb.tile([P, S], F32, name="gained_err")
-        nc.scalar.activation(gained_err[:], picked_err[:], COPY, scale=gain[:])
-
-        acc = []
+        gained_y = sb.tile([P, S], F32, name="gained_y")
         for i in range(PIECES):
+            cols = slice(i * PIECE, (i + 1) * PIECE)
             picked_words = sb.tile([P, PIECE], U32, name="picked_words%d" % i, align_bytes=64)
             nc.vector.tensor_copy(picked_words[:], word_table[:].bitcast(U32).indirect(entries(offs_sb, i)))
-            acc.append(ps.tile([P, PIECE], F32, name="acc%d" % i))
+            acc = ps.tile([P, PIECE], F32, name="acc%d" % i)
             nc.tensor.matmul_mx(
-                out=acc[i][:],
+                out=acc[:],
                 lhsT=w_codes[:].bitcast(FP8X4),
                 lhsT_scale=w_scales[:],
                 rhs=picked_words[:].bitcast(FP8X4),
-                rhs_scale=picked_scales[:, i * PIECE : (i + 1) * PIECE],
+                rhs_scale=picked_scales[:, cols],
                 start=True,
                 stop=True,
             )
+            nc.scalar.activation(gained_y[:, cols], acc[:], COPY, scale=gain[:])
 
-        gained = [sb.tile([P, PIECE], F32, name="gained%d" % i) for i in range(PIECES)]
-        linear = [sb.tile([P, PIECE], F32, name="linear%d" % i) for i in range(PIECES)]
-        clamped = [sb.tile([P, PIECE], F32, name="clamped%d" % i) for i in range(PIECES)]
+        picked_err = sb.tile([P, S], F32, name="picked_err")
         for i in range(PIECES):
             cols = slice(i * PIECE, (i + 1) * PIECE)
-            nc.vector.scalar_tensor_tensor(gained[i][:], acc[i][:], gain[:], gained_err[:, cols], ALU.mult, ALU.add)
-        nc.scalar.activation(linear[0][:], gained[0][:], COPY, scale=back[:])
-        nc.vector.tensor_scalar(clamped[0][:], gained[0][:], lower[:], upper[:], ALU.max, ALU.min)
-        below_upper = sb.tile([P, PIECE], F32, name="below_upper")
-        nc.scalar.activation(linear[1][:], gained[1][:], IDENTITY, scale=back[:], bias=lower[:])
-        nc.scalar.activation(below_upper[:], gained[1][:], RELU, scale=-1.0, bias=upper[:])
-        nc.scalar.activation(clamped[1][:], below_upper[:], RELU, scale=-1.0, bias=width[:])
+            nc.vector.tensor_copy(picked_err[:, cols], memory[:].indirect(entries(slot_sb, i)))
+
+        gained = sb.tile([P, S], F32, name="gained")
+        linear = sb.tile([P, S], F32, name="linear")
+        clamped = sb.tile([P, S], F32, name="clamped")
         for i in range(PIECES):
-            nc.vector.tensor_tensor(memory[:].indirect(entries(slot_sb, i)), clamped[i][:], linear[i][:], ALU.add)
+            cols = slice(i * PIECE, (i + 1) * PIECE)
+            nc.vector.scalar_tensor_tensor(gained[:, cols], picked_err[:, cols], gain[:], gained_y[:, cols], ALU.mult, ALU.add)
+            nc.scalar.activation(linear[:, cols], gained[:, cols], COPY, scale=back[:])
+        for i in range(PIECES):
+            cols = slice(i * PIECE, (i + 1) * PIECE)
+            nc.vector.tensor_scalar(clamped[:, cols], gained[:, cols], lower[:], upper[:], ALU.max, ALU.min)
+        nc.vector.tensor_tensor(memory[:].indirect(slot_sb[:]), clamped[:], linear[:], ALU.add)
 
         nc.sync.dma_start(out=out, in_=memory[:])

@@ -45,9 +45,9 @@ def tile_picked_yerrfb_put_p_kernel(tc, x_words, x_scales, w1, err, thr, offs, s
         for r in range(4):
             nc.sync.dma_start(out=scale_table[r:P:32, :].bitcast(I32), in_=x_scales[0, r:16:4, :].bitcast(I32))
         nc.sync.dma_start(out=word_table[:, WORDS_AHEAD:], in_=words_hbm[:, WORDS_AHEAD:])
+        nc.sync.dma_start(out=thr_sb[:], in_=thr)
         nc.sync.dma_start(slot_sb[:], slot)
         nc.sync.dma_start(out=memory[:], in_=err)
-        nc.gpsimd.dma_start(out=thr_sb[:], in_=thr)
 
         upper = sb.tile([P, 1], F32, name="upper")
         lower = sb.tile([P, 1], F32, name="lower")

from contextlib import ExitStack

import concourse.mybir as mybir

K, T, S, N, U = 512, 2048, 512, 128, 1024
FLOPS = 2 * K * N * S

F32 = mybir.dt.float32
BF16 = mybir.dt.bfloat16
I32 = mybir.dt.int32
U32 = mybir.dt.uint32
U16 = mybir.dt.uint16
U8 = mybir.dt.uint8
FP8X4 = mybir.dt.float8_e4m3fn_x4
ALU = mybir.AluOpType
COPY = mybir.ActivationFunctionType.Copy

P = 128
PACK = 4
PIECES = 2
PIECE = S // PIECES
SEND_GAIN = 1.2
WORDS_AHEAD = 512


def tile_picked_yerrfb_put_p_kernel(tc, x_words, x_scales, w1, err, thr, offs, slot, out):
    nc = tc.nc
    with ExitStack() as ctx:
        sb = ctx.enter_context(tc.tile_pool(name="sb", bufs=1))
        ps = ctx.enter_context(tc.psum_pool(name="ps", bufs=1))

        offs_sb = sb.tile([P, S // 16], U16, name="offs_sb")
        slot_sb = sb.tile([P, S // 16], U16, name="slot_sb")
        scale_table = sb.tile([P, T], U8, name="scale_table", align_bytes=64)
        word_table = sb.tile([P, T], I32, name="word_table", align_bytes=64)
        w_raw = sb.tile([P, PACK, N], F32, name="w_raw")
        memory = sb.tile([P, U], F32, name="memory", align_bytes=64)
        thr_sb = sb.tile([P, 1], F32, name="thr_sb")

        nc.vector.memset(scale_table[:].bitcast(I32), 0)
        words_hbm = x_words[0].rearrange("p c t -> p (c t)").bitcast(I32)
        nc.sync.dma_start(offs_sb[:], offs)
        nc.sync.dma_start(out=w_raw[:], in_=w1.rearrange("(p j) n -> p j n", j=PACK))
        nc.sync.dma_start(out=word_table[:, :WORDS_AHEAD], in_=words_hbm[:, :WORDS_AHEAD])
        for r in range(4):
            nc.sync.dma_start(out=scale_table[r:P:32, :].bitcast(I32), in_=x_scales[0, r:16:4, :].bitcast(I32))
        nc.sync.dma_start(out=word_table[:, WORDS_AHEAD:], in_=words_hbm[:, WORDS_AHEAD:])
        nc.sync.dma_start(out=thr_sb[:], in_=thr)
        nc.sync.dma_start(slot_sb[:], slot)
        nc.sync.dma_start(out=memory[:], in_=err)

        upper = sb.tile([P, 1], F32, name="upper")
        lower = sb.tile([P, 1], F32, name="lower")
        half_sign = sb.tile([P, 1], F32, name="half_sign")
        gain = sb.tile([P, 1], F32, name="gain")
        back = sb.tile([P, 1], F32, name="back")
        nc.gpsimd.tensor_scalar(half_sign[:], thr_sb[:], 0.0, 0.5, ALU.is_gt, ALU.subtract)
        nc.scalar.activation(gain[:], half_sign[:], COPY, scale=-2.0 * SEND_GAIN)
        nc.scalar.activation(back[:], half_sign[:], COPY, scale=2.0 * (SEND_GAIN - 1.0) / SEND_GAIN)
        nc.scalar.activation(lower[:], thr_sb[:], COPY, scale=gain[:])
        nc.scalar.activation(upper[:], lower[:], COPY, scale=-1.0)

        picked_scales = sb.tile([P, S], U8, name="picked_scales", align_bytes=64)
        nc.vector.tensor_copy(picked_scales[:], scale_table[:].indirect(offs_sb[:]))

        w_grouped = sb.tile([P, N, PACK], BF16, name="w_grouped", align_bytes=64)
        nc.scalar.activation(w_grouped[:], w_raw[:].rearrange("p j n -> p n j"), COPY)
        w_codes = sb.tile([P, N], U32, name="w_codes", align_bytes=64)
        w_scales = sb.tile([P, N], U8, name="w_scales", align_bytes=64)
        nc.vector.quantize_mx(out=w_codes[:].bitcast(FP8X4), scales=w_scales[:], in_=w_grouped[:].rearrange("p n j -> p (n j)"))

        def entries(lst, i):
            return lst[:, i * PIECE // 16 : (i + 1) * PIECE // 16]

        gained_y = sb.tile([P, S], F32, name="gained_y")
        for i in range(PIECES):
            cols = slice(i * PIECE, (i + 1) * PIECE)
            picked_words = sb.tile([P, PIECE], U32, name="picked_words%d" % i, align_bytes=64)
            nc.vector.tensor_copy(picked_words[:], word_table[:].bitcast(U32).indirect(entries(offs_sb, i)))
            acc = ps.tile([P, PIECE], F32, name="acc%d" % i)
            nc.tensor.matmul_mx(
                out=acc[:],
                lhsT=w_codes[:].bitcast(FP8X4),
                lhsT_scale=w_scales[:],
                rhs=picked_words[:].bitcast(FP8X4),
                rhs_scale=picked_scales[:, cols],
                start=True,
                stop=True,
            )
            nc.scalar.activation(gained_y[:, cols], acc[:], COPY, scale=gain[:])

        picked_err = sb.tile([P, S], F32, name="picked_err")
        for i in range(PIECES):
            cols = slice(i * PIECE, (i + 1) * PIECE)
            nc.vector.tensor_copy(picked_err[:, cols], memory[:].indirect(entries(slot_sb, i)))

        gained = sb.tile([P, S], F32, name="gained")
        linear = sb.tile([P, S], F32, name="linear")
        clamped = sb.tile([P, S], F32, name="clamped")
        for i in range(PIECES):
            cols = slice(i * PIECE, (i + 1) * PIECE)
            nc.vector.scalar_tensor_tensor(gained[:, cols], picked_err[:, cols], gain[:], gained_y[:, cols], ALU.mult, ALU.add)
            nc.scalar.activation(linear[:, cols], gained[:, cols], COPY, scale=back[:])
        for i in range(PIECES):
            cols = slice(i * PIECE, (i + 1) * PIECE)
            nc.vector.tensor_scalar(clamped[:, cols], gained[:, cols], lower[:], upper[:], ALU.max, ALU.min)
        nc.vector.tensor_tensor(memory[:].indirect(slot_sb[:]), clamped[:], linear[:], ALU.add)

        nc.sync.dma_start(out=out, in_=memory[:])
